import numpy as np
import ml_dtypes


def mxq(x, axis, fmt="e4m3"):
    dtype, down = {"e4m3": (ml_dtypes.float8_e4m3fn, 7), "e5m2": (ml_dtypes.float8_e5m2, 14)}[fmt]
    v = np.moveaxis(np.asarray(x, np.float32).astype(ml_dtypes.bfloat16).astype(np.float64), axis, -1)
    blocks = v.reshape(v.shape[:-1] + (-1, 32))
    amax = np.abs(blocks).max(-1, keepdims=True)
    byte = np.maximum(np.where(amax > 0, np.frexp(amax)[1] - 1 + 127, 0) - down, 1)
    scale = np.exp2(byte - 127.0)
    codes = (blocks / scale).astype(np.float32).astype(dtype).astype(np.float64)
    return np.moveaxis((codes * scale).reshape(v.shape), -1, axis)


WIDE = False


def mx_kscale(k):
    if not WIDE:
        return np.ones(k)
    levels = np.array([10, -10, 5, -5, 0])
    if k % 512:
        return np.exp2(np.random.permutation(np.resize(levels, k // 32))).repeat(32)
    a = np.empty((k // 512, 16))
    for p in range(k // 512):
        a[p, :8] = np.random.permutation(np.resize(levels, 8))
        for g in range(8):
            far = levels[np.abs(levels - a[p, g]) >= 10]
            a[p, g + 8] = far[np.random.randint(len(far))]
    return np.exp2(a.ravel()).repeat(32)


def f64(x):
    return np.asarray(x).astype(np.float64)


def striped(idx):
    return np.tile(idx.reshape(-1, 16).T, (8, 1)).astype(np.uint16)


def unstriped(offs):
    return offs[:16].T.reshape(-1).astype(np.int64)


def pack_weight(w):
    k, n = w.shape
    w = f64(np.asarray(w, np.float32).astype(ml_dtypes.bfloat16)).reshape(k // 32, 32, n)
    amax = np.abs(w).max(1)
    byte = np.clip(np.where(amax > 0, np.frexp(amax)[1] - 1 + 127 - 7, 1), 1, 254)
    scaled = (w * np.exp2(127.0 - byte)[:, None, :]).reshape(k, n).astype(np.float32)
    words = np.ascontiguousarray(scaled.reshape(k // 512, 128, 4, n).transpose(0, 1, 3, 2)).astype(ml_dtypes.float8_e4m3fn).view(np.uint8)
    return words, np.ascontiguousarray(byte.astype(np.uint8).reshape(k // 512, 16, n))


def unpack_weight(words, scales):
    g, p, n, _ = words.shape
    vals = np.ascontiguousarray(words).view(ml_dtypes.float8_e4m3fn).astype(np.float64) * np.repeat(np.exp2(scales.astype(np.float64) - 127.0), 8, axis=1)[..., None]
    return vals.transpose(0, 1, 3, 2).reshape(g * 512, n)


def planes(y):
    n, m = y.shape
    v = y.astype(np.float32).astype(ml_dtypes.bfloat16).astype(np.float64).reshape(n // 32, 32, m)
    top = np.abs(v).max(1)
    byte = np.clip(np.where(top > 0, np.frexp(top)[1] - 1 + 127 - 7, 1), 1, 254)
    codes = (v * np.exp2(127.0 - byte)[:, None, :]).reshape(n, m).astype(np.float32).astype(ml_dtypes.float8_e4m3fn).view(np.uint8)
    words = codes.reshape(n // 512, 128, 4, m).transpose(0, 1, 3, 2)
    return np.ascontiguousarray(words), np.ascontiguousarray(byte.astype(np.uint8).reshape(n // 512, 16, m))


K, T, S, V, N, D = 1024, 2048, 512, 256, 512, 2
P = 2 ** 7


def setup_inputs():
    n = np.random.standard_normal
    s = mx_kscale(K)[:, None]
    packed_xT = pack_weight(n((K, T)) * s)
    return {
        "x_words": packed_xT[0],
        "x_scales": packed_xT[1],
        "w1": (n((K, N)) / np.sqrt(K) / s).astype(np.float32),
        "near": (np.tile(-np.random.uniform(0.0, 1.0, (D, 1, V)), (1, P, 1))).astype(np.float32),
        "sharp": (-np.random.uniform(0.2, 1.0, (N, 1))).astype(np.float32),
        "offs": striped(np.random.permutation(T)[:S]),
        "cen": striped(np.random.permutation(S)[:V]),
        "pos1": striped(np.random.permutation(S)[:V]),
        "pos2": striped(np.random.permutation(S)[:V]),
    }


def reference(x_words, x_scales, w1, near, sharp, offs, cen, pos1, pos2):
    xq = unpack_weight(x_words, x_scales)[:, unstriped(offs)]
    h = mxq(f64(w1), 0, "e4m3").T @ xq
    h0 = h[:, unstriped(pos1)]
    hc = h[:, unstriped(cen)]
    wt0 = np.exp(f64(sharp) * ((h0 - hc) ** 2) + f64(near)[0, :1])
    h1 = h[:, unstriped(pos2)]
    wt1 = np.exp(f64(sharp) * ((h1 - hc) ** 2) + f64(near)[1, :1])
    num = h0 * wt0 + h1 * wt1 + hc
    den = wt0 + wt1 + 1.0
    out_0 = num / den
    return (out_0,) + planes(out_0)

@@ -1,0 +1,204 @@
+from contextlib import ExitStack
+
+import concourse.mybir as mybir
+from concourse.masks import make_identity
+
+F32 = mybir.dt.float32
+BF16 = mybir.dt.bfloat16
+I32 = mybir.dt.int32
+U32 = mybir.dt.uint32
+U16 = mybir.dt.uint16
+U8 = mybir.dt.uint8
+FP8X4 = mybir.dt.float8_e4m3fn_x4
+ACT = mybir.ActivationFunctionType
+ALU = mybir.AluOpType
+
+K, T, S, V, N, D = 1024, 2048, 512, 256, 512, 2
+P = 128
+PACK = 4
+K_PASS = P * PACK
+PASSES = K // K_PASS
+HALVES = V // P
+QUADS = 4
+
+FLOPS = 2 * K * N * S
+
+
+def tile_picked_ybilat_smooth_po_kernel(
+    tc, x_words, x_scales, w1, near, sharp, offs, cen, pos1, pos2, out_0, out_1, out_2
+):
+    nc = tc.nc
+    with ExitStack() as ctx:
+        keep = ctx.enter_context(tc.tile_pool(name="keep", bufs=1))
+        psum = ctx.enter_context(tc.psum_pool(name="psum", bufs=1))
+
+        w_raw = [keep.tile([P, PACK, N], F32, name=f"w_raw{g}") for g in range(PASSES)]
+        x_win = [keep.tile([P, T], I32, name=f"x_win{g}") for g in range(PASSES)]
+        offs_sb = keep.tile([P, S // 16], U16, name="offs_sb")
+        cen_sb = keep.tile([P, V // 16], U16, name="cen_sb")
+        pos_sb = [keep.tile([P, V // 16], U16, name=f"pos_sb{d}") for d in range(D)]
+
+        def load_w(g):
+            rows = w1[g * K_PASS : (g + 1) * K_PASS, :]
+            nc.sync.dma_start(out=w_raw[g][:], in_=rows.rearrange("(p j) n -> p j n", j=PACK))
+
+        xs_win = keep.tile([P, T], U8, name="xs_win")
+        near_row = keep.tile([P, D, V], F32, name="near_row")
+        sharp_sb = keep.tile([P, PACK], F32, name="sharp_sb")
+        nc.gpsimd.memset(near_row[:], 0.0)
+        nc.vector.memset(xs_win[:].bitcast(I32), 0)
+
+        load_w(0)
+        nc.sync.dma_start(out=offs_sb[:], in_=offs)
+        nc.sync.dma_start(out=sharp_sb[:], in_=sharp.rearrange("(p t) o -> p (t o)", t=PACK))
+        nc.sync.dma_start(out=near_row[0:1, :, :], in_=near[:, 0:1, :].rearrange("d o v -> o d v"))
+        load_w(1)
+        for q in range(QUADS):
+            nc.sync.dma_start(
+                out=xs_win[32 * q : 32 * q + 4 * PASSES, :].bitcast(I32),
+                in_=x_scales[:, 4 * q : 4 * q + 4, :].bitcast(I32),
+            )
+        for g in range(PASSES):
+            nc.sync.dma_start(
+                out=x_win[g][:], in_=x_words[g].rearrange("p c r -> p (c r)").bitcast(I32)
+            )
+        nc.sync.dma_start(out=cen_sb[:], in_=cen)
+        for d, pos in enumerate((pos1, pos2)):
+            nc.sync.dma_start(out=pos_sb[d][:], in_=pos)
+
+        ident = keep.tile([P, P], F32, name="ident")
+        make_identity(nc, ident[:])
+
+        minus_sharp = keep.tile([P, PACK], F32, name="minus_sharp")
+        one_half = keep.tile([P, PACK], F32, name="one_half")
+        root = keep.tile([P, PACK], F32, name="root")
+        nc.gpsimd.memset(one_half[:], 0.5)
+        nc.gpsimd.tensor_scalar(minus_sharp[:], sharp_sb[:], -1.0, 0.0, ALU.mult, ALU.add)
+        nc.gpsimd.tensor_tensor(root[:], minus_sharp[:], one_half[:], ALU.pow)
+
+        near_ps = psum.tile([P, D * HALVES, P], F32, name="near_ps", tag="den0")
+        for d in range(D):
+            for u in range(HALVES):
+                nc.tensor.transpose(near_ps[:, d * HALVES + u, :], near_row[:, d, u * P : (u + 1) * P], ident[:])
+        near_col = keep.tile([P, D * HALVES], F32, name="near_col", tag="near_then_recip")
+        nc.scalar.copy(near_col[:], near_ps[:, :, 0])
+
+        xs = keep.tile([P, S], U8, name="xs", align_bytes=64)
+        nc.vector.tensor_copy(xs[:], xs_win[:].indirect(offs_sb[:]))
+        w_codes, w_scales = [], []
+        for g in range(PASSES):
+            w_bf = keep.tile([P, PACK * P * PACK], BF16, name=f"w_bf{g}", align_bytes=64)
+            dst = w_bf[:].rearrange("p (t m j) -> p m t j", t=PACK, j=PACK)
+            src = w_raw[g][:].rearrange("p j (m t) -> p m t j", t=PACK)
+            if g == 0:
+                nc.scalar.copy(dst, src)
+            else:
+                nc.scalar.copy(dst[:, :48], src[:, :48])
+                nc.vector.tensor_copy(dst[:, 48:], src[:, 48:])
+            codes = keep.tile([P, N], U32, name=f"w_codes{g}", align_bytes=64)
+            scales = keep.tile([P, N], U8, name=f"w_scales{g}", align_bytes=64)
+            nc.vector.quantize_mx(codes[:].bitcast(FP8X4), scales[:], w_bf[:])
+            w_codes.append(codes)
+            w_scales.append(scales)
+        x_codes = [keep.tile([P, S], U32, name=f"x_codes{g}", align_bytes=64) for g in range(PASSES)]
+        half = S // 2
+        nc.vector.tensor_copy(x_codes[0][:], x_win[0][:].bitcast(U32).indirect(offs_sb[:]))
+        for a in range(2):
+            nc.vector.tensor_copy(
+                x_codes[1][:, a * half : (a + 1) * half],
+                x_win[1][:].bitcast(U32).indirect(offs_sb[:, a * half // 16 : (a + 1) * half // 16]),
+            )
+
+        pieces = [(0, 0, half, "bank0"), (0, half, S, "sq1")]
+        pieces.extend((t, 0, S, f"bank{t}") for t in range(1, PACK))
+        h_ps = [psum.tile([P, b - a], F32, name=f"h_ps{t}_{a}", tag=bank) for t, a, b, bank in pieces]
+        for g in range(PASSES):
+            for acc, (t, a, b, bank) in zip(h_ps, pieces):
+                cols = slice(t * P, (t + 1) * P)
+                nc.tensor.matmul_mx(
+                    out=acc[:],
+                    lhsT=w_codes[g][:, cols].bitcast(FP8X4),
+                    lhsT_scale=w_scales[g][:, cols],
+                    rhs=x_codes[g][:, a:b].bitcast(FP8X4),
+                    rhs_scale=xs[4 * g :, a:b],
+                    start=(g == 0),
+                    stop=(g == PASSES - 1),
+                )
+        h = [keep.tile([P, S], F32, name=f"h{t}") for t in range(PACK)]
+        for acc, (t, a, b, bank) in zip(h_ps, pieces):
+            if a:
+                nc.vector.tensor_copy(h[t][:, a:b], acc[:])
+            else:
+                nc.scalar.copy(h[t][:, a:b], acc[:])
+
+        def turn(dst, src, start=True, stop=True):
+            nc.tensor.matmul(dst, src, ident[:], start=start, stop=stop, is_transpose=True)
+
+        centre, diff_ps, wt, den_sq = [], [], [], []
+        for t in range(PACK):
+            hc = keep.tile([P, V], F32, name=f"hc{t}")
+            nc.vector.tensor_copy(hc[:], h[t][:].indirect(cen_sb[:]))
+            sq_ps = psum.tile([P, D * HALVES, P], F32, name=f"sq_ps{t}", tag=f"sq{t % 2}")
+            df_ps = psum.tile([P, D * HALVES, P], F32, name=f"df_ps{t}", tag=f"bank{t}")
+            wt_t = keep.tile([P, D * HALVES, P], F32, name=f"wt{t}")
+            diffs = []
+            for d in range(D):
+                diff = keep.tile([P, V], F32, name=f"diff{t}_{d}")
+                nc.vector.tensor_tensor(diff[:], h[t][:].indirect(pos_sb[d][:]), hc[:], ALU.subtract)
+                sq = keep.tile([P, V], F32, name=f"sq{t}_{d}")
+                nc.scalar.activation(sq[:], diff[:], ACT.Square, scale=root[:, t : t + 1])
+                for u in range(HALVES):
+                    turn(sq_ps[:, d * HALVES + u, :], sq[:, u * P : (u + 1) * P])
+                diffs.append(diff)
+            for c in range(D * HALVES):
+                nc.scalar.activation(wt_t[:, c, :], sq_ps[:, c, :], ACT.Exp, bias=near_col[:, c : c + 1], scale=-1.0)
+            den_ps = psum.tile([P, HALVES, P], F32, name=f"den_ps{t}", tag=f"den{(t + 1) % 2}")
+            for u in range(HALVES):
+                for d in range(D):
+                    turn(den_ps[:, u, :], wt_t[:, d * HALVES + u, :], d == 0, d == D - 1)
+            for d in range(D):
+                for u in range(HALVES):
+                    turn(df_ps[:, d * HALVES + u, :], diffs[d][:, u * P : (u + 1) * P])
+            dsq = keep.tile([P, V], F32, name=f"den_sq{t}")
+            nc.scalar.activation(dsq[:], den_ps[:].rearrange("p u v -> p (u v)"), ACT.Square, bias=1.0)
+            centre.append(hc)
+            diff_ps.append(df_ps)
+            wt.append(wt_t)
+            den_sq.append(dsq)
+
+        recip = keep.tile([P, PACK, V], F32, name="recip", tag="near_then_recip")
+        num_ps = []
+        for t in range(PACK):
+            pull = keep.tile([P, D * HALVES, P], F32, name=f"pull{t}")
+            nc.vector.tensor_tensor(pull[:], diff_ps[t][:], wt[t][:], ALU.mult)
+            num = psum.tile([P, HALVES, P], F32, name=f"num_ps{t}", tag=f"bank{t}")
+            for u in range(HALVES):
+                for d in range(D):
+                    turn(num[:, u, :], pull[:, d * HALVES + u, :], d == 0, d == D - 1)
+            num_ps.append(num)
+
+        y = keep.tile([P, PACK, V], F32, name="y")
+        out_rows = out_0.rearrange("(p t) v -> p t v", t=PACK)
+        for t in range(PACK):
+            nc.scalar.activation(recip[:, t, :], den_sq[t][:], ACT.Abs_reciprocal_sqrt)
+            shift = keep.tile([P, V], F32, name=f"shift{t}")
+            nc.vector.tensor_tensor(shift[:], num_ps[t][:].rearrange("p u v -> p (u v)"), recip[:, t, :], ALU.mult)
+            nc.vector.tensor_tensor(y[:, t, :], shift[:], centre[t][:], ALU.add)
+            nc.sync.dma_start(out=out_rows[:, t, :], in_=y[:, t, :])
+
+        y_bf = keep.tile([P, V * PACK], BF16, name="y_bf", align_bytes=64)
+        y_codes = keep.tile([P, V], U32, name="y_codes", align_bytes=64)
+        y_scales = keep.tile([P, V], U8, name="y_scales", align_bytes=64)
+        dst = y_bf[:].rearrange("p (c i t) -> p c t i", i=4, t=PACK)
+        src = y[:].rearrange("p t (c i) -> p c t i", i=4)
+        cut = V // 8
+        nc.scalar.copy(dst[:, :cut], src[:, :cut])
+        nc.vector.tensor_copy(dst[:, cut:], src[:, cut:])
+        nc.vector.quantize_mx(y_codes[:].bitcast(FP8X4), y_scales[:], y_bf[:])
+        nc.sync.dma_start(out=out_1[0].rearrange("p c r -> p (c r)").bitcast(I32), in_=y_codes[:].bitcast(I32))
+        for q in range(QUADS):
+            queue = nc.sync if q % 2 else nc.scalar
+            queue.dma_start(
+                out=out_2[0, 4 * q : 4 * q + 4, :].bitcast(I32),
+                in_=y_scales[32 * q : 32 * q + 4, :].bitcast(I32),
+            )

@@ -42,6 +42,11 @@ def tile_picked_ybilat_smooth_po_kernel(
             rows = w1[g * K_PASS : (g + 1) * K_PASS, :]
             nc.sync.dma_start(out=w_raw[g][:], in_=rows.rearrange("(p j) n -> p j n", j=PACK))
 
+        def load_x(g):
+            nc.sync.dma_start(
+                out=x_win[g][:], in_=x_words[g].rearrange("p c r -> p (c r)").bitcast(I32)
+            )
+
         xs_win = keep.tile([P, T], U8, name="xs_win")
         near_row = keep.tile([P, D, V], F32, name="near_row")
         sharp_sb = keep.tile([P, PACK], F32, name="sharp_sb")
@@ -49,19 +54,17 @@ def tile_picked_ybilat_smooth_po_kernel(
         nc.vector.memset(xs_win[:].bitcast(I32), 0)
 
         load_w(0)
-        nc.sync.dma_start(out=offs_sb[:], in_=offs)
-        nc.sync.dma_start(out=sharp_sb[:], in_=sharp.rearrange("(p t) o -> p (t o)", t=PACK))
         nc.sync.dma_start(out=near_row[0:1, :, :], in_=near[:, 0:1, :].rearrange("d o v -> o d v"))
-        load_w(1)
+        nc.sync.dma_start(out=offs_sb[:], in_=offs)
         for q in range(QUADS):
             nc.sync.dma_start(
                 out=xs_win[32 * q : 32 * q + 4 * PASSES, :].bitcast(I32),
                 in_=x_scales[:, 4 * q : 4 * q + 4, :].bitcast(I32),
             )
-        for g in range(PASSES):
-            nc.sync.dma_start(
-                out=x_win[g][:], in_=x_words[g].rearrange("p c r -> p (c r)").bitcast(I32)
-            )
+        load_x(0)
+        load_w(1)
+        load_x(1)
+        nc.sync.dma_start(out=sharp_sb[:], in_=sharp.rearrange("(p t) o -> p (t o)", t=PACK))
         nc.sync.dma_start(out=cen_sb[:], in_=cen)
         for d, pos in enumerate((pos1, pos2)):
             nc.sync.dma_start(out=pos_sb[d][:], in_=pos)
@@ -82,27 +85,27 @@ def tile_picked_ybilat_smooth_po_kernel(
                 nc.tensor.transpose(near_ps[:, d * HALVES + u, :], near_row[:, d, u * P : (u + 1) * P], ident[:])
         near_col = keep.tile([P, D * HALVES], F32, name="near_col", tag="near_then_recip")
         nc.scalar.copy(near_col[:], near_ps[:, :, 0])
+        near_spare = keep.tile([P, D * HALVES], F32, name="near_spare", tag="near_then_square")
+        nc.scalar.copy(near_spare[:], near_ps[:, :, 0])
 
         xs = keep.tile([P, S], U8, name="xs", align_bytes=64)
         nc.vector.tensor_copy(xs[:], xs_win[:].indirect(offs_sb[:]))
+        x_codes = [keep.tile([P, S], U32, name=f"x_codes{g}", align_bytes=64) for g in range(PASSES)]
+        half = S // 2
         w_codes, w_scales = [], []
         for g in range(PASSES):
             w_bf = keep.tile([P, PACK * P * PACK], BF16, name=f"w_bf{g}", align_bytes=64)
             dst = w_bf[:].rearrange("p (t m j) -> p m t j", t=PACK, j=PACK)
             src = w_raw[g][:].rearrange("p j (m t) -> p m t j", t=PACK)
-            if g == 0:
-                nc.scalar.copy(dst, src)
-            else:
-                nc.scalar.copy(dst[:, :48], src[:, :48])
-                nc.vector.tensor_copy(dst[:, 48:], src[:, 48:])
+            nc.scalar.copy(dst[:, :48], src[:, :48])
+            nc.vector.tensor_copy(dst[:, 48:], src[:, 48:])
             codes = keep.tile([P, N], U32, name=f"w_codes{g}", align_bytes=64)
             scales = keep.tile([P, N], U8, name=f"w_scales{g}", align_bytes=64)
             nc.vector.quantize_mx(codes[:].bitcast(FP8X4), scales[:], w_bf[:])
             w_codes.append(codes)
             w_scales.append(scales)
-        x_codes = [keep.tile([P, S], U32, name=f"x_codes{g}", align_bytes=64) for g in range(PASSES)]
-        half = S // 2
-        nc.vector.tensor_copy(x_codes[0][:], x_win[0][:].bitcast(U32).indirect(offs_sb[:]))
+            if g == 0:
+                nc.vector.tensor_copy(x_codes[0][:], x_win[0][:].bitcast(U32).indirect(offs_sb[:]))
         for a in range(2):
             nc.vector.tensor_copy(
                 x_codes[1][:, a * half : (a + 1) * half],
@@ -124,7 +127,7 @@ def tile_picked_ybilat_smooth_po_kernel(
                     start=(g == 0),
                     stop=(g == PASSES - 1),
                 )
-        h = [keep.tile([P, S], F32, name=f"h{t}") for t in range(PACK)]
+        h = [keep.tile([P, S], F32, name=f"h{t}", tag=f"h{t}") for t in range(PACK)]
         for acc, (t, a, b, bank) in zip(h_ps, pieces):
             if a:
                 nc.vector.tensor_copy(h[t][:, a:b], acc[:])
@@ -134,56 +137,99 @@ def tile_picked_ybilat_smooth_po_kernel(
         def turn(dst, src, start=True, stop=True):
             nc.tensor.matmul(dst, src, ident[:], start=start, stop=stop, is_transpose=True)
 
-        centre, diff_ps, wt, den_sq = [], [], [], []
-        for t in range(PACK):
-            hc = keep.tile([P, V], F32, name=f"hc{t}")
-            nc.vector.tensor_copy(hc[:], h[t][:].indirect(cen_sb[:]))
-            sq_ps = psum.tile([P, D * HALVES, P], F32, name=f"sq_ps{t}", tag=f"sq{t % 2}")
-            df_ps = psum.tile([P, D * HALVES, P], F32, name=f"df_ps{t}", tag=f"bank{t}")
-            wt_t = keep.tile([P, D * HALVES, P], F32, name=f"wt{t}")
-            diffs = []
-            for d in range(D):
-                diff = keep.tile([P, V], F32, name=f"diff{t}_{d}")
-                nc.vector.tensor_tensor(diff[:], h[t][:].indirect(pos_sb[d][:]), hc[:], ALU.subtract)
-                sq = keep.tile([P, V], F32, name=f"sq{t}_{d}")
-                nc.scalar.activation(sq[:], diff[:], ACT.Square, scale=root[:, t : t + 1])
-                for u in range(HALVES):
-                    turn(sq_ps[:, d * HALVES + u, :], sq[:, u * P : (u + 1) * P])
-                diffs.append(diff)
-            for c in range(D * HALVES):
-                nc.scalar.activation(wt_t[:, c, :], sq_ps[:, c, :], ACT.Exp, bias=near_col[:, c : c + 1], scale=-1.0)
-            den_ps = psum.tile([P, HALVES, P], F32, name=f"den_ps{t}", tag=f"den{(t + 1) % 2}")
+        steps = PACK * D
+        hc = [keep.tile([P, V], F32, name=f"hc{t}") for t in range(PACK)]
+        wt = [keep.tile([P, D * HALVES, P], F32, name=f"wt{t}") for t in range(PACK)]
+        den_sq = [keep.tile([P, V], F32, name=f"den_sq{t}") for t in range(PACK)]
+        diff = [keep.tile([P, V], F32, name=f"diff{s}") for s in range(steps)]
+        sq = {}
+        sq_ps, df_ps, den_ps = {}, {}, {}
+
+        def gather_and_square(s, halves, bank):
+            t, d = divmod(s, D)
+            a, b = halves[0] * P, (halves[-1] + 1) * P
+            window = h[t][:].indirect(pos_sb[d][:, a // 16 : b // 16])
+            nc.vector.tensor_tensor(diff[s][:, a:b], window, hc[t][:, a:b], ALU.subtract)
+            if a == 0:
+                tag = "near_then_square" if s == steps - 1 else f"sq{s}"
+                sq[s] = keep.tile([P, V], F32, name=f"sq{s}", tag=tag)
+            nc.scalar.activation(sq[s][:, a:b], diff[s][:, a:b], ACT.Square, scale=root[:, t : t + 1])
+            turned = psum.tile([P, len(halves), P], F32, name=f"sq_ps{s}_{a}", tag=bank)
+            for i, u in enumerate(halves):
+                turn(turned[:, i, :], sq[s][:, u * P : (u + 1) * P])
+                sq_ps[s, u] = turned[:, i, :]
+
+        def weigh(s):
+            t, d = divmod(s, D)
             for u in range(HALVES):
-                for d in range(D):
-                    turn(den_ps[:, u, :], wt_t[:, d * HALVES + u, :], d == 0, d == D - 1)
-            for d in range(D):
+                c = d * HALVES + u
+                bias = near_spare if s == steps - 3 else near_col
+                nc.scalar.activation(wt[t][:, c, :], sq_ps[s, u], ACT.Exp, bias=bias[:, c : c + 1], scale=-1.0)
+            if d == 0:
+                df_ps[t] = psum.tile([P, D * HALVES, P], F32, name=f"df_ps{t}", tag=f"bank{t}")
+                for e in range(D):
+                    for u in range(HALVES):
+                        turn(df_ps[t][:, e * HALVES + u, :], diff[D * t + e][:, u * P : (u + 1) * P])
+            else:
+                if t % 2 == 0:
+                    den_ps[t // 2] = psum.tile([P, 2, V], F32, name=f"den_ps{t}", tag=f"den{t // 2}")
                 for u in range(HALVES):
-                    turn(df_ps[:, d * HALVES + u, :], diffs[d][:, u * P : (u + 1) * P])
-            dsq = keep.tile([P, V], F32, name=f"den_sq{t}")
-            nc.scalar.activation(dsq[:], den_ps[:].rearrange("p u v -> p (u v)"), ACT.Square, bias=1.0)
-            centre.append(hc)
-            diff_ps.append(df_ps)
-            wt.append(wt_t)
-            den_sq.append(dsq)
+                    for e in range(D):
+                        turn(den_ps[t // 2][:, t % 2, u * P : (u + 1) * P], wt[t][:, e * HALVES + u, :], e == 0, e == D - 1)
+
+        def square_den(t):
+            nc.scalar.activation(den_sq[t][:], den_ps[t // 2][:, t % 2, :], ACT.Square, bias=1.0)
+
+        for s in range(steps):
+            t, d = divmod(s, D)
+            if d == 0:
+                nc.vector.tensor_copy(hc[t][:], h[t][:].indirect(cen_sb[:]))
+            if s == steps - 1:
+                gather_and_square(s, [0], "sq1")
+                gather_and_square(s, [1], "sq0")
+            else:
+                gather_and_square(s, [0, 1], f"sq{t % 2}" if d else f"bank{t}")
+            if s:
+                weigh(s - 1)
+            if d and t:
+                square_den(t - 1)
+        weigh(steps - 1)
 
         recip = keep.tile([P, PACK, V], F32, name="recip", tag="near_then_recip")
         num_ps = []
+        early = PACK - 1
+        late = keep.tile([P, PACK * D * V + early * V], F32, name="late", tag=f"h{PACK - 1}")
+        pull = late[:, : PACK * D * V].rearrange("p (t c m) -> p t c m", t=PACK, m=P)
+        own = late[:, PACK * D * V :].rearrange("p (t v) -> p t v", v=V)
         for t in range(PACK):
-            pull = keep.tile([P, D * HALVES, P], F32, name=f"pull{t}")
-            nc.vector.tensor_tensor(pull[:], diff_ps[t][:], wt[t][:], ALU.mult)
-            num = psum.tile([P, HALVES, P], F32, name=f"num_ps{t}", tag=f"bank{t}")
+            nc.vector.tensor_tensor(pull[:, t], df_ps[t][:], wt[t][:], ALU.mult)
+            num = psum.tile([P, V], F32, name=f"num_ps{t}", tag=f"bank{t}")
             for u in range(HALVES):
                 for d in range(D):
-                    turn(num[:, u, :], pull[:, d * HALVES + u, :], d == 0, d == D - 1)
+                    turn(num[:, u * P : (u + 1) * P], pull[:, t, d * HALVES + u, :], d == 0, d == D - 1)
             num_ps.append(num)
+        total = keep.tile([P, early, V], F32, name="total")
+        for t in range(early):
+            nc.vector.scalar_tensor_tensor(own[:, t, :], den_ps[t // 2][:, t % 2, :], 1.0, hc[t][:], ALU.add, ALU.mult)
+        for t in range(early):
+            nc.vector.tensor_tensor(total[:, t, :], num_ps[t][:], own[:, t, :], ALU.add)
+
+        for t in (0, 1, 3, 2):
+            nc.scalar.activation(recip[:, t, :], den_sq[t][:], ACT.Abs_reciprocal_sqrt)
+            if t == 0:
+                square_den(PACK - 1)
 
         y = keep.tile([P, PACK, V], F32, name="y")
         out_rows = out_0.rearrange("(p t) v -> p t v", t=PACK)
+        shift = keep.tile([P, V], F32, name="shift")
+        last = PACK - 1
         for t in range(PACK):
-            nc.scalar.activation(recip[:, t, :], den_sq[t][:], ACT.Abs_reciprocal_sqrt)
-            shift = keep.tile([P, V], F32, name=f"shift{t}")
-            nc.vector.tensor_tensor(shift[:], num_ps[t][:].rearrange("p u v -> p (u v)"), recip[:, t, :], ALU.mult)
-            nc.vector.tensor_tensor(y[:, t, :], shift[:], centre[t][:], ALU.add)
+            if t == last - 1:
+                nc.vector.tensor_tensor(shift[:], num_ps[last][:], recip[:, last, :], ALU.mult)
+            if t < early:
+                nc.vector.tensor_tensor(y[:, t, :], total[:, t, :], recip[:, t, :], ALU.mult)
+            else:
+                nc.vector.tensor_tensor(y[:, t, :], shift[:], hc[t][:], ALU.add)
             nc.sync.dma_start(out=out_rows[:, t, :], in_=y[:, t, :])
 
         y_bf = keep.tile([P, V * PACK], BF16, name="y_bf", align_bytes=64)
@@ -191,7 +237,7 @@ def tile_picked_ybilat_smooth_po_kernel(
         y_scales = keep.tile([P, V], U8, name="y_scales", align_bytes=64)
         dst = y_bf[:].rearrange("p (c i t) -> p c t i", i=4, t=PACK)
         src = y[:].rearrange("p t (c i) -> p c t i", i=4)
-        cut = V // 8
+        cut = 22
         nc.scalar.copy(dst[:, :cut], src[:, :cut])
         nc.vector.tensor_copy(dst[:, cut:], src[:, cut:])
         nc.vector.quantize_mx(y_codes[:].bitcast(FP8X4), y_scales[:], y_bf[:])

@@ -20,6 +20,10 @@ K_PASS = P * PACK
 PASSES = K // K_PASS
 HALVES = V // P
 QUADS = 4
+GROUP = 16
+RUN = 4
+W_SCALAR = 48
+Y_SCALAR = 22
 
 FLOPS = 2 * K * N * S
 
@@ -34,9 +38,9 @@ def tile_picked_ybilat_smooth_po_kernel(
 
         w_raw = [keep.tile([P, PACK, N], F32, name=f"w_raw{g}") for g in range(PASSES)]
         x_win = [keep.tile([P, T], I32, name=f"x_win{g}") for g in range(PASSES)]
-        offs_sb = keep.tile([P, S // 16], U16, name="offs_sb")
-        cen_sb = keep.tile([P, V // 16], U16, name="cen_sb")
-        pos_sb = [keep.tile([P, V // 16], U16, name=f"pos_sb{d}") for d in range(D)]
+        offs_sb = keep.tile([P, S // GROUP], U16, name="offs_sb")
+        cen_sb = keep.tile([P, V // GROUP], U16, name="cen_sb")
+        pos_sb = [keep.tile([P, V // GROUP], U16, name=f"pos_sb{d}") for d in range(D)]
 
         def load_w(g):
             rows = w1[g * K_PASS : (g + 1) * K_PASS, :]
@@ -95,10 +99,10 @@ def tile_picked_ybilat_smooth_po_kernel(
         w_codes, w_scales = [], []
         for g in range(PASSES):
             w_bf = keep.tile([P, PACK * P * PACK], BF16, name=f"w_bf{g}", align_bytes=64)
-            dst = w_bf[:].rearrange("p (t m j) -> p m t j", t=PACK, j=PACK)
-            src = w_raw[g][:].rearrange("p j (m t) -> p m t j", t=PACK)
-            nc.scalar.copy(dst[:, :48], src[:, :48])
-            nc.vector.tensor_copy(dst[:, 48:], src[:, 48:])
+            w_dst = w_bf[:].rearrange("p (t m j) -> p m t j", t=PACK, j=PACK)
+            w_src = w_raw[g][:].rearrange("p j (m t) -> p m t j", t=PACK)
+            nc.scalar.copy(w_dst[:, :W_SCALAR], w_src[:, :W_SCALAR])
+            nc.vector.tensor_copy(w_dst[:, W_SCALAR:], w_src[:, W_SCALAR:])
             codes = keep.tile([P, N], U32, name=f"w_codes{g}", align_bytes=64)
             scales = keep.tile([P, N], U8, name=f"w_scales{g}", align_bytes=64)
             nc.vector.quantize_mx(codes[:].bitcast(FP8X4), scales[:], w_bf[:])
@@ -106,10 +110,10 @@ def tile_picked_ybilat_smooth_po_kernel(
             w_scales.append(scales)
             if g == 0:
                 nc.vector.tensor_copy(x_codes[0][:], x_win[0][:].bitcast(U32).indirect(offs_sb[:]))
-        for a in range(2):
+        for i in range(2):
             nc.vector.tensor_copy(
-                x_codes[1][:, a * half : (a + 1) * half],
-                x_win[1][:].bitcast(U32).indirect(offs_sb[:, a * half // 16 : (a + 1) * half // 16]),
+                x_codes[1][:, i * half : (i + 1) * half],
+                x_win[1][:].bitcast(U32).indirect(offs_sb[:, i * half // GROUP : (i + 1) * half // GROUP]),
             )
 
         pieces = [(0, 0, half, "bank0"), (0, half, S, "sq1")]
@@ -138,6 +142,8 @@ def tile_picked_ybilat_smooth_po_kernel(
             nc.tensor.matmul(dst, src, ident[:], start=start, stop=stop, is_transpose=True)
 
         steps = PACK * D
+        last_step = steps - 1
+        last_tile = PACK - 1
         hc = [keep.tile([P, V], F32, name=f"hc{t}") for t in range(PACK)]
         wt = [keep.tile([P, D * HALVES, P], F32, name=f"wt{t}") for t in range(PACK)]
         den_sq = [keep.tile([P, V], F32, name=f"den_sq{t}") for t in range(PACK)]
@@ -145,13 +151,16 @@ def tile_picked_ybilat_smooth_po_kernel(
         sq = {}
         sq_ps, df_ps, den_ps = {}, {}, {}
 
+        def gather_centres(t):
+            nc.vector.tensor_copy(hc[t][:], h[t][:].indirect(cen_sb[:]))
+
         def gather_and_square(s, halves, bank):
             t, d = divmod(s, D)
             a, b = halves[0] * P, (halves[-1] + 1) * P
-            window = h[t][:].indirect(pos_sb[d][:, a // 16 : b // 16])
-            nc.vector.tensor_tensor(diff[s][:, a:b], window, hc[t][:, a:b], ALU.subtract)
+            neighbours = h[t][:].indirect(pos_sb[d][:, a // GROUP : b // GROUP])
+            nc.vector.tensor_tensor(diff[s][:, a:b], neighbours, hc[t][:, a:b], ALU.subtract)
             if a == 0:
-                tag = "near_then_square" if s == steps - 1 else f"sq{s}"
+                tag = "near_then_square" if s == last_step else f"sq{s}"
                 sq[s] = keep.tile([P, V], F32, name=f"sq{s}", tag=tag)
             nc.scalar.activation(sq[s][:, a:b], diff[s][:, a:b], ACT.Square, scale=root[:, t : t + 1])
             turned = psum.tile([P, len(halves), P], F32, name=f"sq_ps{s}_{a}", tag=bank)
@@ -163,7 +172,7 @@ def tile_picked_ybilat_smooth_po_kernel(
             t, d = divmod(s, D)
             for u in range(HALVES):
                 c = d * HALVES + u
-                bias = near_spare if s == steps - 3 else near_col
+                bias = near_spare if s == last_step - D else near_col
                 nc.scalar.activation(wt[t][:, c, :], sq_ps[s, u], ACT.Exp, bias=bias[:, c : c + 1], scale=-1.0)
             if d == 0:
                 df_ps[t] = psum.tile([P, D * HALVES, P], F32, name=f"df_ps{t}", tag=f"bank{t}")
@@ -180,11 +189,12 @@ def tile_picked_ybilat_smooth_po_kernel(
         def square_den(t):
             nc.scalar.activation(den_sq[t][:], den_ps[t // 2][:, t % 2, :], ACT.Square, bias=1.0)
 
+        gather_centres(0)
         for s in range(steps):
             t, d = divmod(s, D)
-            if d == 0:
-                nc.vector.tensor_copy(hc[t][:], h[t][:].indirect(cen_sb[:]))
-            if s == steps - 1:
+            if d and t < last_tile:
+                gather_centres(t + 1)
+            if s == last_step:
                 gather_and_square(s, [0], "sq1")
                 gather_and_square(s, [1], "sq0")
             else:
@@ -193,12 +203,11 @@ def tile_picked_ybilat_smooth_po_kernel(
                 weigh(s - 1)
             if d and t:
                 square_den(t - 1)
-        weigh(steps - 1)
+        weigh(last_step)
 
         recip = keep.tile([P, PACK, V], F32, name="recip", tag="near_then_recip")
         num_ps = []
-        early = PACK - 1
-        late = keep.tile([P, PACK * D * V + early * V], F32, name="late", tag=f"h{PACK - 1}")
+        late = keep.tile([P, PACK * D * V + last_tile * V], F32, name="late", tag=f"h{last_tile}")
         pull = late[:, : PACK * D * V].rearrange("p (t c m) -> p t c m", t=PACK, m=P)
         own = late[:, PACK * D * V :].rearrange("p (t v) -> p t v", v=V)
         for t in range(PACK):
@@ -208,25 +217,24 @@ def tile_picked_ybilat_smooth_po_kernel(
                 for d in range(D):
                     turn(num[:, u * P : (u + 1) * P], pull[:, t, d * HALVES + u, :], d == 0, d == D - 1)
             num_ps.append(num)
-        total = keep.tile([P, early, V], F32, name="total")
-        for t in range(early):
+        total = keep.tile([P, last_tile, V], F32, name="total")
+        for t in range(last_tile):
             nc.vector.scalar_tensor_tensor(own[:, t, :], den_ps[t // 2][:, t % 2, :], 1.0, hc[t][:], ALU.add, ALU.mult)
-        for t in range(early):
+        for t in range(last_tile):
             nc.vector.tensor_tensor(total[:, t, :], num_ps[t][:], own[:, t, :], ALU.add)
 
         for t in (0, 1, 3, 2):
             nc.scalar.activation(recip[:, t, :], den_sq[t][:], ACT.Abs_reciprocal_sqrt)
             if t == 0:
-                square_den(PACK - 1)
+                square_den(last_tile)
 
         y = keep.tile([P, PACK, V], F32, name="y")
         out_rows = out_0.rearrange("(p t) v -> p t v", t=PACK)
         shift = keep.tile([P, V], F32, name="shift")
-        last = PACK - 1
         for t in range(PACK):
-            if t == last - 1:
-                nc.vector.tensor_tensor(shift[:], num_ps[last][:], recip[:, last, :], ALU.mult)
-            if t < early:
+            if t == last_tile - 1:
+                nc.vector.tensor_tensor(shift[:], num_ps[last_tile][:], recip[:, last_tile, :], ALU.mult)
+            if t < last_tile:
                 nc.vector.tensor_tensor(y[:, t, :], total[:, t, :], recip[:, t, :], ALU.mult)
             else:
                 nc.vector.tensor_tensor(y[:, t, :], shift[:], hc[t][:], ALU.add)
@@ -235,11 +243,10 @@ def tile_picked_ybilat_smooth_po_kernel(
         y_bf = keep.tile([P, V * PACK], BF16, name="y_bf", align_bytes=64)
         y_codes = keep.tile([P, V], U32, name="y_codes", align_bytes=64)
         y_scales = keep.tile([P, V], U8, name="y_scales", align_bytes=64)
-        dst = y_bf[:].rearrange("p (c i t) -> p c t i", i=4, t=PACK)
-        src = y[:].rearrange("p t (c i) -> p c t i", i=4)
-        cut = 22
-        nc.scalar.copy(dst[:, :cut], src[:, :cut])
-        nc.vector.tensor_copy(dst[:, cut:], src[:, cut:])
+        y_dst = y_bf[:].rearrange("p (c i t) -> p c t i", i=RUN, t=PACK)
+        y_src = y[:].rearrange("p t (c i) -> p c t i", i=RUN)
+        nc.scalar.copy(y_dst[:, :Y_SCALAR], y_src[:, :Y_SCALAR])
+        nc.vector.tensor_copy(y_dst[:, Y_SCALAR:], y_src[:, Y_SCALAR:])
         nc.vector.quantize_mx(y_codes[:].bitcast(FP8X4), y_scales[:], y_bf[:])
         nc.sync.dma_start(out=out_1[0].rearrange("p c r -> p (c r)").bitcast(I32), in_=y_codes[:].bitcast(I32))
         for q in range(QUADS):

from contextlib import ExitStack

import concourse.mybir as mybir
from concourse.masks import make_identity

F32 = mybir.dt.float32
BF16 = mybir.dt.bfloat16
I32 = mybir.dt.int32
U32 = mybir.dt.uint32
U16 = mybir.dt.uint16
U8 = mybir.dt.uint8
FP8X4 = mybir.dt.float8_e4m3fn_x4
ACT = mybir.ActivationFunctionType
ALU = mybir.AluOpType

K, T, S, V, N, D = 1024, 2048, 512, 256, 512, 2
P = 128
PACK = 4
K_PASS = P * PACK
PASSES = K // K_PASS
HALVES = V // P
QUADS = 4
GROUP = 16
RUN = 4
W_SCALAR = 48
Y_SCALAR = 22

FLOPS = 2 * K * N * S


def tile_picked_ybilat_smooth_po_kernel(
    tc, x_words, x_scales, w1, near, sharp, offs, cen, pos1, pos2, out_0, out_1, out_2
):
    nc = tc.nc
    with ExitStack() as ctx:
        keep = ctx.enter_context(tc.tile_pool(name="keep", bufs=1))
        psum = ctx.enter_context(tc.psum_pool(name="psum", bufs=1))

        w_raw = [keep.tile([P, PACK, N], F32, name=f"w_raw{g}") for g in range(PASSES)]
        x_win = [keep.tile([P, T], I32, name=f"x_win{g}") for g in range(PASSES)]
        offs_sb = keep.tile([P, S // GROUP], U16, name="offs_sb")
        cen_sb = keep.tile([P, V // GROUP], U16, name="cen_sb")
        pos_sb = [keep.tile([P, V // GROUP], U16, name=f"pos_sb{d}") for d in range(D)]

        def load_w(g):
            rows = w1[g * K_PASS : (g + 1) * K_PASS, :]
            nc.sync.dma_start(out=w_raw[g][:], in_=rows.rearrange("(p j) n -> p j n", j=PACK))

        def load_x(g):
            nc.sync.dma_start(
                out=x_win[g][:], in_=x_words[g].rearrange("p c r -> p (c r)").bitcast(I32)
            )

        xs_win = keep.tile([P, T], U8, name="xs_win")
        near_row = keep.tile([P, D, V], F32, name="near_row")
        sharp_sb = keep.tile([P, PACK], F32, name="sharp_sb")
        nc.gpsimd.memset(near_row[:], 0.0)
        nc.vector.memset(xs_win[:].bitcast(I32), 0)

        load_w(0)
        nc.sync.dma_start(out=near_row[0:1, :, :], in_=near[:, 0:1, :].rearrange("d o v -> o d v"))
        nc.sync.dma_start(out=offs_sb[:], in_=offs)
        for q in range(QUADS):
            nc.sync.dma_start(
                out=xs_win[32 * q : 32 * q + 4 * PASSES, :].bitcast(I32),
                in_=x_scales[:, 4 * q : 4 * q + 4, :].bitcast(I32),
            )
        load_x(0)
        load_w(1)
        load_x(1)
        nc.sync.dma_start(out=sharp_sb[:], in_=sharp.rearrange("(p t) o -> p (t o)", t=PACK))
        nc.sync.dma_start(out=cen_sb[:], in_=cen)
        for d, pos in enumerate((pos1, pos2)):
            nc.sync.dma_start(out=pos_sb[d][:], in_=pos)

        ident = keep.tile([P, P], F32, name="ident")
        make_identity(nc, ident[:])

        minus_sharp = keep.tile([P, PACK], F32, name="minus_sharp")
        one_half = keep.tile([P, PACK], F32, name="one_half")
        root = keep.tile([P, PACK], F32, name="root")
        nc.gpsimd.memset(one_half[:], 0.5)
        nc.gpsimd.tensor_scalar(minus_sharp[:], sharp_sb[:], -1.0, 0.0, ALU.mult, ALU.add)
        nc.gpsimd.tensor_tensor(root[:], minus_sharp[:], one_half[:], ALU.pow)

        near_ps = psum.tile([P, D * HALVES, P], F32, name="near_ps", tag="den0")
        for d in range(D):
            for u in range(HALVES):
                nc.tensor.transpose(near_ps[:, d * HALVES + u, :], near_row[:, d, u * P : (u + 1) * P], ident[:])
        near_col = keep.tile([P, D * HALVES], F32, name="near_col", tag="near_then_recip")
        nc.scalar.copy(near_col[:], near_ps[:, :, 0])
        near_spare = keep.tile([P, D * HALVES], F32, name="near_spare", tag="near_then_square")
        nc.scalar.copy(near_spare[:], near_ps[:, :, 0])

        xs = keep.tile([P, S], U8, name="xs", align_bytes=64)
        nc.vector.tensor_copy(xs[:], xs_win[:].indirect(offs_sb[:]))
        x_codes = [keep.tile([P, S], U32, name=f"x_codes{g}", align_bytes=64) for g in range(PASSES)]
        half = S // 2
        w_codes, w_scales = [], []
        for g in range(PASSES):
            w_bf = keep.tile([P, PACK * P * PACK], BF16, name=f"w_bf{g}", align_bytes=64)
            w_dst = w_bf[:].rearrange("p (t m j) -> p m t j", t=PACK, j=PACK)
            w_src = w_raw[g][:].rearrange("p j (m t) -> p m t j", t=PACK)
            nc.scalar.copy(w_dst[:, :W_SCALAR], w_src[:, :W_SCALAR])
            nc.vector.tensor_copy(w_dst[:, W_SCALAR:], w_src[:, W_SCALAR:])
            codes = keep.tile([P, N], U32, name=f"w_codes{g}", align_bytes=64)
            scales = keep.tile([P, N], U8, name=f"w_scales{g}", align_bytes=64)
            nc.vector.quantize_mx(codes[:].bitcast(FP8X4), scales[:], w_bf[:])
            w_codes.append(codes)
            w_scales.append(scales)
            if g == 0:
                nc.vector.tensor_copy(x_codes[0][:], x_win[0][:].bitcast(U32).indirect(offs_sb[:]))
        for i in range(2):
            nc.vector.tensor_copy(
                x_codes[1][:, i * half : (i + 1) * half],
                x_win[1][:].bitcast(U32).indirect(offs_sb[:, i * half // GROUP : (i + 1) * half // GROUP]),
            )

        pieces = [(0, 0, half, "bank0"), (0, half, S, "sq1")]
        pieces.extend((t, 0, S, f"bank{t}") for t in range(1, PACK))
        h_ps = [psum.tile([P, b - a], F32, name=f"h_ps{t}_{a}", tag=bank) for t, a, b, bank in pieces]
        for g in range(PASSES):
            for acc, (t, a, b, bank) in zip(h_ps, pieces):
                cols = slice(t * P, (t + 1) * P)
                nc.tensor.matmul_mx(
                    out=acc[:],
                    lhsT=w_codes[g][:, cols].bitcast(FP8X4),
                    lhsT_scale=w_scales[g][:, cols],
                    rhs=x_codes[g][:, a:b].bitcast(FP8X4),
                    rhs_scale=xs[4 * g :, a:b],
                    start=(g == 0),
                    stop=(g == PASSES - 1),
                )
        h = [keep.tile([P, S], F32, name=f"h{t}", tag=f"h{t}") for t in range(PACK)]
        for acc, (t, a, b, bank) in zip(h_ps, pieces):
            if a:
                nc.vector.tensor_copy(h[t][:, a:b], acc[:])
            else:
                nc.scalar.copy(h[t][:, a:b], acc[:])

        def turn(dst, src, start=True, stop=True):
            nc.tensor.matmul(dst, src, ident[:], start=start, stop=stop, is_transpose=True)

        steps = PACK * D
        last_step = steps - 1
        last_tile = PACK - 1
        hc = [keep.tile([P, V], F32, name=f"hc{t}") for t in range(PACK)]
        wt = [keep.tile([P, D * HALVES, P], F32, name=f"wt{t}") for t in range(PACK)]
        den_sq = [keep.tile([P, V], F32, name=f"den_sq{t}") for t in range(PACK)]
        diff = [keep.tile([P, V], F32, name=f"diff{s}") for s in range(steps)]
        sq = {}
        sq_ps, df_ps, den_ps = {}, {}, {}

        def gather_centres(t):
            nc.vector.tensor_copy(hc[t][:], h[t][:].indirect(cen_sb[:]))

        def gather_and_square(s, halves, bank):
            t, d = divmod(s, D)
            a, b = halves[0] * P, (halves[-1] + 1) * P
            neighbours = h[t][:].indirect(pos_sb[d][:, a // GROUP : b // GROUP])
            nc.vector.tensor_tensor(diff[s][:, a:b], neighbours, hc[t][:, a:b], ALU.subtract)
            if a == 0:
                tag = "near_then_square" if s == last_step else f"sq{s}"
                sq[s] = keep.tile([P, V], F32, name=f"sq{s}", tag=tag)
            nc.scalar.activation(sq[s][:, a:b], diff[s][:, a:b], ACT.Square, scale=root[:, t : t + 1])
            turned = psum.tile([P, len(halves), P], F32, name=f"sq_ps{s}_{a}", tag=bank)
            for i, u in enumerate(halves):
                turn(turned[:, i, :], sq[s][:, u * P : (u + 1) * P])
                sq_ps[s, u] = turned[:, i, :]

        def weigh(s):
            t, d = divmod(s, D)
            for u in range(HALVES):
                c = d * HALVES + u
                bias = near_spare if s == last_step - D else near_col
                nc.scalar.activation(wt[t][:, c, :], sq_ps[s, u], ACT.Exp, bias=bias[:, c : c + 1], scale=-1.0)
            if d == 0:
                df_ps[t] = psum.tile([P, D * HALVES, P], F32, name=f"df_ps{t}", tag=f"bank{t}")
                for e in range(D):
                    for u in range(HALVES):
                        turn(df_ps[t][:, e * HALVES + u, :], diff[D * t + e][:, u * P : (u + 1) * P])
            else:
                if t % 2 == 0:
                    den_ps[t // 2] = psum.tile([P, 2, V], F32, name=f"den_ps{t}", tag=f"den{t // 2}")
                for u in range(HALVES):
                    for e in range(D):
                        turn(den_ps[t // 2][:, t % 2, u * P : (u + 1) * P], wt[t][:, e * HALVES + u, :], e == 0, e == D - 1)

        def square_den(t):
            nc.scalar.activation(den_sq[t][:], den_ps[t // 2][:, t % 2, :], ACT.Square, bias=1.0)

        gather_centres(0)
        for s in range(steps):
            t, d = divmod(s, D)
            if d and t < last_tile:
                gather_centres(t + 1)
            if s == last_step:
                gather_and_square(s, [0], "sq1")
                gather_and_square(s, [1], "sq0")
            else:
                gather_and_square(s, [0, 1], f"sq{t % 2}" if d else f"bank{t}")
            if s:
                weigh(s - 1)
            if d and t:
                square_den(t - 1)
        weigh(last_step)

        recip = keep.tile([P, PACK, V], F32, name="recip", tag="near_then_recip")
        num_ps = []
        late = keep.tile([P, PACK * D * V + last_tile * V], F32, name="late", tag=f"h{last_tile}")
        pull = late[:, : PACK * D * V].rearrange("p (t c m) -> p t c m", t=PACK, m=P)
        own = late[:, PACK * D * V :].rearrange("p (t v) -> p t v", v=V)
        for t in range(PACK):
            nc.vector.tensor_tensor(pull[:, t], df_ps[t][:], wt[t][:], ALU.mult)
            num = psum.tile([P, V], F32, name=f"num_ps{t}", tag=f"bank{t}")
            for u in range(HALVES):
                for d in range(D):
                    turn(num[:, u * P : (u + 1) * P], pull[:, t, d * HALVES + u, :], d == 0, d == D - 1)
            num_ps.append(num)
        total = keep.tile([P, last_tile, V], F32, name="total")
        for t in range(last_tile):
            nc.vector.scalar_tensor_tensor(own[:, t, :], den_ps[t // 2][:, t % 2, :], 1.0, hc[t][:], ALU.add, ALU.mult)
        for t in range(last_tile):
            nc.vector.tensor_tensor(total[:, t, :], num_ps[t][:], own[:, t, :], ALU.add)

        for t in (0, 1, 3, 2):
            nc.scalar.activation(recip[:, t, :], den_sq[t][:], ACT.Abs_reciprocal_sqrt)
            if t == 0:
                square_den(last_tile)

        y = keep.tile([P, PACK, V], F32, name="y")
        out_rows = out_0.rearrange("(p t) v -> p t v", t=PACK)
        shift = keep.tile([P, V], F32, name="shift")
        for t in range(PACK):
            if t == last_tile - 1:
                nc.vector.tensor_tensor(shift[:], num_ps[last_tile][:], recip[:, last_tile, :], ALU.mult)
            if t < last_tile:
                nc.vector.tensor_tensor(y[:, t, :], total[:, t, :], recip[:, t, :], ALU.mult)
            else:
                nc.vector.tensor_tensor(y[:, t, :], shift[:], hc[t][:], ALU.add)
            nc.sync.dma_start(out=out_rows[:, t, :], in_=y[:, t, :])

        y_bf = keep.tile([P, V * PACK], BF16, name="y_bf", align_bytes=64)
        y_codes = keep.tile([P, V], U32, name="y_codes", align_bytes=64)
        y_scales = keep.tile([P, V], U8, name="y_scales", align_bytes=64)
        y_dst = y_bf[:].rearrange("p (c i t) -> p c t i", i=RUN, t=PACK)
        y_src = y[:].rearrange("p t (c i) -> p c t i", i=RUN)
        nc.scalar.copy(y_dst[:, :Y_SCALAR], y_src[:, :Y_SCALAR])
        nc.vector.tensor_copy(y_dst[:, Y_SCALAR:], y_src[:, Y_SCALAR:])
        nc.vector.quantize_mx(y_codes[:].bitcast(FP8X4), y_scales[:], y_bf[:])
        nc.sync.dma_start(out=out_1[0].rearrange("p c r -> p (c r)").bitcast(I32), in_=y_codes[:].bitcast(I32))
        for q in range(QUADS):
            queue = nc.sync if q % 2 else nc.scalar
            queue.dma_start(
                out=out_2[0, 4 * q : 4 * q + 4, :].bitcast(I32),
                in_=y_scales[32 * q : 32 * q + 4, :].bitcast(I32),
            )
